import numpy as np
import ml_dtypes


def mxq(x, axis, fmt="e4m3"):
    dtype, down = {"e4m3": (ml_dtypes.float8_e4m3fn, 7), "e5m2": (ml_dtypes.float8_e5m2, 14)}[fmt]
    v = np.moveaxis(np.asarray(x, np.float32).astype(ml_dtypes.bfloat16).astype(np.float64), axis, -1)
    blocks = v.reshape(v.shape[:-1] + (-1, 32))
    amax = np.abs(blocks).max(-1, keepdims=True)
    byte = np.maximum(np.where(amax > 0, np.frexp(amax)[1] - 1 + 127, 0) - down, 1)
    scale = np.exp2(byte - 127.0)
    codes = (blocks / scale).astype(np.float32).astype(dtype).astype(np.float64)
    return np.moveaxis((codes * scale).reshape(v.shape), -1, axis)


WIDE = False


def mx_kscale(k):
    if not WIDE:
        return np.ones(k)
    levels = np.array([10, -10, 5, -5, 0])
    if k % 512:
        return np.exp2(np.random.permutation(np.resize(levels, k // 32))).repeat(32)
    a = np.empty((k // 512, 16))
    for p in range(k // 512):
        a[p, :8] = np.random.permutation(np.resize(levels, 8))
        for g in range(8):
            far = levels[np.abs(levels - a[p, g]) >= 10]
            a[p, g + 8] = far[np.random.randint(len(far))]
    return np.exp2(a.ravel()).repeat(32)


def f64(x):
    return np.asarray(x).astype(np.float64)


def striped(idx):
    return np.tile(idx.reshape(-1, 16).T, (8, 1)).astype(np.uint16)


def unstriped(offs):
    return offs[:16].T.reshape(-1).astype(np.int64)


def pack_weight(w):
    k, n = w.shape
    w = f64(np.asarray(w, np.float32).astype(ml_dtypes.bfloat16)).reshape(k // 32, 32, n)
    amax = np.abs(w).max(1)
    byte = np.clip(np.where(amax > 0, np.frexp(amax)[1] - 1 + 127 - 7, 1), 1, 254)
    scaled = (w * np.exp2(127.0 - byte)[:, None, :]).reshape(k, n).astype(np.float32)
    words = np.ascontiguousarray(scaled.reshape(k // 512, 128, 4, n).transpose(0, 1, 3, 2)).astype(ml_dtypes.float8_e4m3fn).view(np.uint8)
    return words, np.ascontiguousarray(byte.astype(np.uint8).reshape(k // 512, 16, n))


def unpack_weight(words, scales):
    g, p, n, _ = words.shape
    vals = np.ascontiguousarray(words).view(ml_dtypes.float8_e4m3fn).astype(np.float64) * np.repeat(np.exp2(scales.astype(np.float64) - 127.0), 8, axis=1)[..., None]
    return vals.transpose(0, 1, 3, 2).reshape(g * 512, n)


K, T, S, N, U, R = 512, 1024, 512, 128, 1024, 256


def setup_inputs():
    n = np.random.standard_normal
    s = mx_kscale(K)[:, None]
    packed_xT = pack_weight(n((K, T)) * s)
    return {
        "x_words": packed_xT[0],
        "x_scales": packed_xT[1],
        "w1": (n((K, N)) / np.sqrt(K) / s).astype(np.float32),
        "lev": (n((N, U))).astype(np.float32),
        "tre": (0.4 * n((N, U))).astype(np.float32),
        "seas": (np.random.uniform(0.6, 1.5, (N, R))).astype(np.float32),
        "alpha": (np.random.uniform(0.2, 0.6, (N, 1))).astype(np.float32),
        "offs": striped(np.random.permutation(T)[:S]),
        "ser": striped(np.random.permutation(U)[:S]),
        "sea": striped(np.random.permutation(np.concatenate([np.arange(R), np.random.randint(0, R, S - R)]))),
    }


def reference(x_words, x_scales, w1, lev, tre, seas, alpha, offs, ser, sea):
    levg = f64(lev)[:, unstriped(ser)]
    treg = f64(tre)[:, unstriped(ser)]
    pred = levg + 0.9 * treg
    xq = unpack_weight(x_words, x_scales)[:, unstriped(offs)]
    y = mxq(f64(w1), 0, "e4m3").T @ xq
    sf = f64(seas)[:, unstriped(sea)]
    err = y / sf - pred
    lnew = pred + f64(alpha) * err
    out = f64(lev).copy()
    out[:, unstriped(ser)] = lnew
    return out

@@ -1,0 +1,109 @@
+import concourse.mybir as mybir
+from contextlib import ExitStack
+
+K, T, S, N, U, R = 512, 1024, 512, 128, 1024, 256
+FLOPS = 2 * K * N * S
+P = 128
+F32 = mybir.dt.float32
+BF16 = mybir.dt.bfloat16
+I32 = mybir.dt.int32
+U32 = mybir.dt.uint32
+U16 = mybir.dt.uint16
+U8 = mybir.dt.uint8
+FP8X4 = mybir.dt.float8_e4m3fn_x4
+ACT = mybir.ActivationFunctionType
+ALU = mybir.AluOpType
+
+
+def tile_picked_yholtw_put_p_kernel(
+    tc, x_words, x_scales, w1, lev, tre, seas, alpha, offs, ser, sea, out
+):
+    nc = tc.nc
+    with ExitStack() as ctx:
+        keep = ctx.enter_context(tc.tile_pool(name="keep", bufs=1))
+        psum = ctx.enter_context(tc.psum_pool(name="psum", bufs=1))
+
+        offs_t = keep.tile([P, S // 16], U16)
+        ser_t = keep.tile([P, S // 16], U16)
+        sea_t = keep.tile([P, S // 16], U16)
+        scale_table = keep.tile([P, T], U8, align_bytes=64)
+        word_table = keep.tile([P, T], U32, align_bytes=64)
+        w_raw = keep.tile([P, 4, N], F32)
+        seas_t = keep.tile([P, R], F32)
+        tre_t = keep.tile([P, U], F32)
+        lev_t = keep.tile([P, U], F32)
+        alpha_t = keep.tile([P, 1], F32)
+
+        nc.vector.memset(scale_table[:].bitcast(I32), 0)
+        nc.sync.dma_start(offs_t[:], offs)
+        for q in range(4):
+            nc.sync.dma_start(
+                scale_table[32 * q : 32 * q + 4, :].bitcast(I32),
+                x_scales[0, 4 * q : 4 * q + 4, :].bitcast(I32),
+            )
+        nc.sync.dma_start(seas_t[:], seas)
+        nc.sync.dma_start(w_raw[:], w1.rearrange("(p j) n -> p j n", j=4))
+        nc.sync.dma_start(
+            word_table[:].bitcast(I32),
+            x_words[0].rearrange("p n t -> p (n t)").bitcast(I32),
+        )
+        nc.sync.dma_start(tre_t[:], tre)
+        nc.sync.dma_start(ser_t[:], ser)
+        nc.sync.dma_start(sea_t[:], sea)
+        nc.sync.dma_start(lev_t[:], lev)
+        nc.gpsimd.dma_start(alpha_t[:], alpha)
+
+        keep_lev = keep.tile([P, 1], F32)
+        keep_tre = keep.tile([P, 1], F32)
+        nc.gpsimd.tensor_scalar(keep_lev[:], alpha_t[:], -1.0, 1.0, ALU.mult, ALU.add)
+        nc.gpsimd.tensor_scalar(keep_tre[:], alpha_t[:], -0.9, 0.9, ALU.mult, ALU.add)
+
+        picked_scales = keep.tile([P, S], U8, align_bytes=64)
+        picked_words = keep.tile([P, S], U32, align_bytes=64)
+        nc.vector.tensor_copy(picked_scales[:], scale_table[:].indirect(offs_t[:]))
+
+        root = keep.tile([P, R], F32)
+        inv_table = keep.tile([P, 3 * R], F32)
+        nc.scalar.activation(root[:], seas_t[:], ACT.Abs_reciprocal_sqrt)
+        nc.scalar.activation(inv_table[:, R : 2 * R], root[:], ACT.Square)
+        nc.scalar.activation(inv_table[:, 2 * R :], seas_t[:], ACT.Sign)
+
+        nc.vector.tensor_tensor(
+            inv_table[:, :R], inv_table[:, R : 2 * R], inv_table[:, 2 * R :], ALU.mult
+        )
+        w_grouped = keep.tile([P, N, 4], BF16, align_bytes=64)
+        w_words = keep.tile([P, N], U32, align_bytes=64)
+        w_scales = keep.tile([P, N], U8, align_bytes=64)
+        nc.scalar.copy(w_grouped[:], w_raw[:].rearrange("p j n -> p n j"))
+        nc.vector.quantize_mx(
+            out=w_words[:].bitcast(FP8X4),
+            scales=w_scales[:],
+            in_=w_grouped[:].rearrange("p n j -> p (n j)"),
+        )
+        nc.vector.tensor_copy(picked_words[:], word_table[:].indirect(offs_t[:]))
+        y_psum = psum.tile([P, S], F32)
+        nc.tensor.matmul_mx(
+            out=y_psum[:],
+            lhsT=w_words[:].bitcast(FP8X4),
+            lhsT_scale=w_scales[:],
+            rhs=picked_words[:].bitcast(FP8X4),
+            rhs_scale=picked_scales[:],
+            start=True,
+            stop=True,
+        )
+        ay = keep.tile([P, S], F32)
+        nc.scalar.activation(ay[:], y_psum[:], ACT.Copy, scale=alpha_t[:])
+
+        tre_picked = keep.tile([P, S], F32)
+        tre_part = keep.tile([P, S], F32)
+        nc.vector.tensor_copy(tre_picked[:], tre_t[:].indirect(ser_t[:]))
+        lev_scaled = keep.tile([P, U], F32)
+        nc.scalar.activation(lev_scaled[:], lev_t[:], ACT.Copy, scale=keep_lev[:])
+        nc.scalar.activation(tre_part[:], tre_picked[:], ACT.Copy, scale=keep_tre[:])
+
+        obs = keep.tile([P, S], F32)
+        nc.vector.tensor_tensor(obs[:], inv_table[:].indirect(sea_t[:]), ay[:], ALU.mult)
+        both = keep.tile([P, S], F32)
+        nc.vector.tensor_tensor(both[:], lev_scaled[:].indirect(ser_t[:]), obs[:], ALU.add)
+        nc.vector.tensor_tensor(lev_t[:].indirect(ser_t[:]), both[:], tre_part[:], ALU.add)
+        nc.sync.dma_start(out, lev_t[:])

@@ -36,41 +36,36 @@ def tile_picked_yholtw_put_p_kernel(
 
         nc.vector.memset(scale_table[:].bitcast(I32), 0)
         nc.sync.dma_start(offs_t[:], offs)
+        nc.sync.dma_start(
+            word_table[:].bitcast(I32),
+            x_words[0].rearrange("p n t -> p (n t)").bitcast(I32),
+        )
         for q in range(4):
             nc.sync.dma_start(
                 scale_table[32 * q : 32 * q + 4, :].bitcast(I32),
                 x_scales[0, 4 * q : 4 * q + 4, :].bitcast(I32),
             )
-        nc.sync.dma_start(seas_t[:], seas)
         nc.sync.dma_start(w_raw[:], w1.rearrange("(p j) n -> p j n", j=4))
-        nc.sync.dma_start(
-            word_table[:].bitcast(I32),
-            x_words[0].rearrange("p n t -> p (n t)").bitcast(I32),
-        )
+        nc.sync.dma_start(seas_t[:], seas)
         nc.sync.dma_start(tre_t[:], tre)
         nc.sync.dma_start(ser_t[:], ser)
         nc.sync.dma_start(sea_t[:], sea)
         nc.sync.dma_start(lev_t[:], lev)
         nc.gpsimd.dma_start(alpha_t[:], alpha)
 
-        keep_lev = keep.tile([P, 1], F32)
+        warm = keep.tile([P, 2], F32)
+        nc.gpsimd.memset(warm[:, 0:1], 1.0)
+        nc.scalar.activation(warm[:, 1:2], warm[:, 0:1], ACT.Abs_reciprocal_sqrt)
+        keep_lev = keep.tile([P, 1], F32, tag="late")
         keep_tre = keep.tile([P, 1], F32)
         nc.gpsimd.tensor_scalar(keep_lev[:], alpha_t[:], -1.0, 1.0, ALU.mult, ALU.add)
         nc.gpsimd.tensor_scalar(keep_tre[:], alpha_t[:], -0.9, 0.9, ALU.mult, ALU.add)
 
         picked_scales = keep.tile([P, S], U8, align_bytes=64)
         picked_words = keep.tile([P, S], U32, align_bytes=64)
+        nc.vector.tensor_copy(picked_words[:], word_table[:].indirect(offs_t[:]))
         nc.vector.tensor_copy(picked_scales[:], scale_table[:].indirect(offs_t[:]))
 
-        root = keep.tile([P, R], F32)
-        inv_table = keep.tile([P, 3 * R], F32)
-        nc.scalar.activation(root[:], seas_t[:], ACT.Abs_reciprocal_sqrt)
-        nc.scalar.activation(inv_table[:, R : 2 * R], root[:], ACT.Square)
-        nc.scalar.activation(inv_table[:, 2 * R :], seas_t[:], ACT.Sign)
-
-        nc.vector.tensor_tensor(
-            inv_table[:, :R], inv_table[:, R : 2 * R], inv_table[:, 2 * R :], ALU.mult
-        )
         w_grouped = keep.tile([P, N, 4], BF16, align_bytes=64)
         w_words = keep.tile([P, N], U32, align_bytes=64)
         w_scales = keep.tile([P, N], U8, align_bytes=64)
@@ -80,25 +75,36 @@ def tile_picked_yholtw_put_p_kernel(
             scales=w_scales[:],
             in_=w_grouped[:].rearrange("p n j -> p (n j)"),
         )
-        nc.vector.tensor_copy(picked_words[:], word_table[:].indirect(offs_t[:]))
-        y_psum = psum.tile([P, S], F32)
-        nc.tensor.matmul_mx(
-            out=y_psum[:],
-            lhsT=w_words[:].bitcast(FP8X4),
-            lhsT_scale=w_scales[:],
-            rhs=picked_words[:].bitcast(FP8X4),
-            rhs_scale=picked_scales[:],
-            start=True,
-            stop=True,
+        halves = [slice(h * (S // 2), (h + 1) * (S // 2)) for h in range(2)]
+        y_banks = [psum.tile([P, S], F32, name="y_bank%d" % h) for h in range(2)]
+        for h in range(2):
+            nc.tensor.matmul_mx(
+                out=y_banks[h][:, : S // 2],
+                lhsT=w_words[:].bitcast(FP8X4),
+                lhsT_scale=w_scales[:],
+                rhs=picked_words[:, halves[h]].bitcast(FP8X4),
+                rhs_scale=picked_scales[:, halves[h]],
+                start=True,
+                stop=True,
+            )
+        sign = keep.tile([P, R], F32, tag="early")
+        inv_table = keep.tile([P, 3 * R], F32)
+        nc.scalar.activation(inv_table[:, 2 * R :], seas_t[:], ACT.Abs_reciprocal_sqrt)
+        nc.scalar.activation(inv_table[:, R : 2 * R], inv_table[:, 2 * R :], ACT.Square)
+        nc.scalar.activation(sign[:], seas_t[:], ACT.Sign)
+
+        nc.vector.tensor_tensor(
+            inv_table[:, :R], inv_table[:, R : 2 * R], sign[:], ALU.mult
         )
         ay = keep.tile([P, S], F32)
-        nc.scalar.activation(ay[:], y_psum[:], ACT.Copy, scale=alpha_t[:])
+        for h in range(2):
+            nc.scalar.activation(ay[:, halves[h]], y_banks[h][:, : S // 2], ACT.Copy, scale=alpha_t[:])
 
-        tre_picked = keep.tile([P, S], F32)
-        tre_part = keep.tile([P, S], F32)
+        tre_picked = keep.tile([P, S], F32, tag="early")
         nc.vector.tensor_copy(tre_picked[:], tre_t[:].indirect(ser_t[:]))
         lev_scaled = keep.tile([P, U], F32)
         nc.scalar.activation(lev_scaled[:], lev_t[:], ACT.Copy, scale=keep_lev[:])
+        tre_part = keep.tile([P, S], F32, tag="late")
         nc.scalar.activation(tre_part[:], tre_picked[:], ACT.Copy, scale=keep_tre[:])
 
         obs = keep.tile([P, S], F32)

@@ -40,32 +40,38 @@ def tile_picked_yholtw_put_p_kernel(
             word_table[:].bitcast(I32),
             x_words[0].rearrange("p n t -> p (n t)").bitcast(I32),
         )
+        nc.sync.dma_start(seas_t[:], seas)
         for q in range(4):
             nc.sync.dma_start(
                 scale_table[32 * q : 32 * q + 4, :].bitcast(I32),
                 x_scales[0, 4 * q : 4 * q + 4, :].bitcast(I32),
             )
         nc.sync.dma_start(w_raw[:], w1.rearrange("(p j) n -> p j n", j=4))
-        nc.sync.dma_start(seas_t[:], seas)
         nc.sync.dma_start(tre_t[:], tre)
-        nc.sync.dma_start(ser_t[:], ser)
+        series = [slice(h * (U // 2), (h + 1) * (U // 2)) for h in range(2)]
+        for cols in series:
+            nc.sync.dma_start(lev_t[:, cols], lev[:, cols])
         nc.sync.dma_start(sea_t[:], sea)
-        nc.sync.dma_start(lev_t[:], lev)
+        nc.sync.dma_start(ser_t[:], ser)
         nc.gpsimd.dma_start(alpha_t[:], alpha)
 
-        warm = keep.tile([P, 2], F32)
-        nc.gpsimd.memset(warm[:, 0:1], 1.0)
-        nc.scalar.activation(warm[:, 1:2], warm[:, 0:1], ACT.Abs_reciprocal_sqrt)
-        keep_lev = keep.tile([P, 1], F32, tag="late")
-        keep_tre = keep.tile([P, 1], F32)
+        keep_lev = keep.tile([P, 1], F32)
         nc.gpsimd.tensor_scalar(keep_lev[:], alpha_t[:], -1.0, 1.0, ALU.mult, ALU.add)
-        nc.gpsimd.tensor_scalar(keep_tre[:], alpha_t[:], -0.9, 0.9, ALU.mult, ALU.add)
 
         picked_scales = keep.tile([P, S], U8, align_bytes=64)
         picked_words = keep.tile([P, S], U32, align_bytes=64)
         nc.vector.tensor_copy(picked_words[:], word_table[:].indirect(offs_t[:]))
         nc.vector.tensor_copy(picked_scales[:], scale_table[:].indirect(offs_t[:]))
 
+        sign = keep.tile([P, R], F32)
+        inv_table = keep.tile([P, 3 * R], F32)
+        nc.scalar.activation(inv_table[:, 2 * R :], seas_t[:], ACT.Abs_reciprocal_sqrt)
+        nc.scalar.activation(inv_table[:, R : 2 * R], inv_table[:, 2 * R :], ACT.Square)
+        nc.scalar.activation(sign[:], seas_t[:], ACT.Sign)
+
+        nc.vector.tensor_tensor(
+            inv_table[:, :R], inv_table[:, R : 2 * R], sign[:], ALU.mult
+        )
         w_grouped = keep.tile([P, N, 4], BF16, align_bytes=64)
         w_words = keep.tile([P, N], U32, align_bytes=64)
         w_scales = keep.tile([P, N], U8, align_bytes=64)
@@ -87,29 +93,19 @@ def tile_picked_yholtw_put_p_kernel(
                 start=True,
                 stop=True,
             )
-        sign = keep.tile([P, R], F32, tag="early")
-        inv_table = keep.tile([P, 3 * R], F32)
-        nc.scalar.activation(inv_table[:, 2 * R :], seas_t[:], ACT.Abs_reciprocal_sqrt)
-        nc.scalar.activation(inv_table[:, R : 2 * R], inv_table[:, 2 * R :], ACT.Square)
-        nc.scalar.activation(sign[:], seas_t[:], ACT.Sign)
-
-        nc.vector.tensor_tensor(
-            inv_table[:, :R], inv_table[:, R : 2 * R], sign[:], ALU.mult
-        )
         ay = keep.tile([P, S], F32)
         for h in range(2):
             nc.scalar.activation(ay[:, halves[h]], y_banks[h][:, : S // 2], ACT.Copy, scale=alpha_t[:])
 
-        tre_picked = keep.tile([P, S], F32, tag="early")
-        nc.vector.tensor_copy(tre_picked[:], tre_t[:].indirect(ser_t[:]))
-        lev_scaled = keep.tile([P, U], F32)
-        nc.scalar.activation(lev_scaled[:], lev_t[:], ACT.Copy, scale=keep_lev[:])
-        tre_part = keep.tile([P, S], F32, tag="late")
-        nc.scalar.activation(tre_part[:], tre_picked[:], ACT.Copy, scale=keep_tre[:])
+        pred = keep.tile([P, U], F32)
+        for cols in series:
+            nc.vector.scalar_tensor_tensor(pred[:, cols], tre_t[:, cols], 0.9, lev_t[:, cols], ALU.mult, ALU.add)
+        pred_kept = keep.tile([P, U], F32)
+        nc.scalar.activation(pred_kept[:], pred[:], ACT.Copy, scale=keep_lev[:])
 
         obs = keep.tile([P, S], F32)
         nc.vector.tensor_tensor(obs[:], inv_table[:].indirect(sea_t[:]), ay[:], ALU.mult)
-        both = keep.tile([P, S], F32)
-        nc.vector.tensor_tensor(both[:], lev_scaled[:].indirect(ser_t[:]), obs[:], ALU.add)
-        nc.vector.tensor_tensor(lev_t[:].indirect(ser_t[:]), both[:], tre_part[:], ALU.add)
+        pred_picked = keep.tile([P, S], F32)
+        nc.vector.tensor_copy(pred_picked[:], pred_kept[:].indirect(ser_t[:]))
+        nc.vector.tensor_tensor(lev_t[:].indirect(ser_t[:]), pred_picked[:], obs[:], ALU.add)
         nc.sync.dma_start(out, lev_t[:])

import concourse.mybir as mybir
from contextlib import ExitStack

K, T, S, N, U, R = 512, 1024, 512, 128, 1024, 256
FLOPS = 2 * K * N * S
P = 128
F32 = mybir.dt.float32
BF16 = mybir.dt.bfloat16
I32 = mybir.dt.int32
U32 = mybir.dt.uint32
U16 = mybir.dt.uint16
U8 = mybir.dt.uint8
FP8X4 = mybir.dt.float8_e4m3fn_x4
ACT = mybir.ActivationFunctionType
ALU = mybir.AluOpType


def tile_picked_yholtw_put_p_kernel(
    tc, x_words, x_scales, w1, lev, tre, seas, alpha, offs, ser, sea, out
):
    nc = tc.nc
    with ExitStack() as ctx:
        keep = ctx.enter_context(tc.tile_pool(name="keep", bufs=1))
        psum = ctx.enter_context(tc.psum_pool(name="psum", bufs=1))

        offs_t = keep.tile([P, S // 16], U16)
        ser_t = keep.tile([P, S // 16], U16)
        sea_t = keep.tile([P, S // 16], U16)
        scale_table = keep.tile([P, T], U8, align_bytes=64)
        word_table = keep.tile([P, T], U32, align_bytes=64)
        w_raw = keep.tile([P, 4, N], F32)
        seas_t = keep.tile([P, R], F32)
        tre_t = keep.tile([P, U], F32)
        lev_t = keep.tile([P, U], F32)
        alpha_t = keep.tile([P, 1], F32)

        nc.vector.memset(scale_table[:].bitcast(I32), 0)
        nc.sync.dma_start(offs_t[:], offs)
        nc.sync.dma_start(
            word_table[:].bitcast(I32),
            x_words[0].rearrange("p n t -> p (n t)").bitcast(I32),
        )
        nc.sync.dma_start(seas_t[:], seas)
        for q in range(4):
            nc.sync.dma_start(
                scale_table[32 * q : 32 * q + 4, :].bitcast(I32),
                x_scales[0, 4 * q : 4 * q + 4, :].bitcast(I32),
            )
        nc.sync.dma_start(w_raw[:], w1.rearrange("(p j) n -> p j n", j=4))
        nc.sync.dma_start(tre_t[:], tre)
        series = [slice(h * (U // 2), (h + 1) * (U // 2)) for h in range(2)]
        for cols in series:
            nc.sync.dma_start(lev_t[:, cols], lev[:, cols])
        nc.sync.dma_start(sea_t[:], sea)
        nc.sync.dma_start(ser_t[:], ser)
        nc.gpsimd.dma_start(alpha_t[:], alpha)

        keep_lev = keep.tile([P, 1], F32)
        nc.gpsimd.tensor_scalar(keep_lev[:], alpha_t[:], -1.0, 1.0, ALU.mult, ALU.add)

        picked_scales = keep.tile([P, S], U8, align_bytes=64)
        picked_words = keep.tile([P, S], U32, align_bytes=64)
        nc.vector.tensor_copy(picked_words[:], word_table[:].indirect(offs_t[:]))
        nc.vector.tensor_copy(picked_scales[:], scale_table[:].indirect(offs_t[:]))

        sign = keep.tile([P, R], F32)
        inv_table = keep.tile([P, 3 * R], F32)
        nc.scalar.activation(inv_table[:, 2 * R :], seas_t[:], ACT.Abs_reciprocal_sqrt)
        nc.scalar.activation(inv_table[:, R : 2 * R], inv_table[:, 2 * R :], ACT.Square)
        nc.scalar.activation(sign[:], seas_t[:], ACT.Sign)

        nc.vector.tensor_tensor(
            inv_table[:, :R], inv_table[:, R : 2 * R], sign[:], ALU.mult
        )
        w_grouped = keep.tile([P, N, 4], BF16, align_bytes=64)
        w_words = keep.tile([P, N], U32, align_bytes=64)
        w_scales = keep.tile([P, N], U8, align_bytes=64)
        nc.scalar.copy(w_grouped[:], w_raw[:].rearrange("p j n -> p n j"))
        nc.vector.quantize_mx(
            out=w_words[:].bitcast(FP8X4),
            scales=w_scales[:],
            in_=w_grouped[:].rearrange("p n j -> p (n j)"),
        )
        halves = [slice(h * (S // 2), (h + 1) * (S // 2)) for h in range(2)]
        y_banks = [psum.tile([P, S], F32, name="y_bank%d" % h) for h in range(2)]
        for h in range(2):
            nc.tensor.matmul_mx(
                out=y_banks[h][:, : S // 2],
                lhsT=w_words[:].bitcast(FP8X4),
                lhsT_scale=w_scales[:],
                rhs=picked_words[:, halves[h]].bitcast(FP8X4),
                rhs_scale=picked_scales[:, halves[h]],
                start=True,
                stop=True,
            )
        ay = keep.tile([P, S], F32)
        for h in range(2):
            nc.scalar.activation(ay[:, halves[h]], y_banks[h][:, : S // 2], ACT.Copy, scale=alpha_t[:])

        pred = keep.tile([P, U], F32)
        for cols in series:
            nc.vector.scalar_tensor_tensor(pred[:, cols], tre_t[:, cols], 0.9, lev_t[:, cols], ALU.mult, ALU.add)
        pred_kept = keep.tile([P, U], F32)
        nc.scalar.activation(pred_kept[:], pred[:], ACT.Copy, scale=keep_lev[:])

        obs = keep.tile([P, S], F32)
        nc.vector.tensor_tensor(obs[:], inv_table[:].indirect(sea_t[:]), ay[:], ALU.mult)
        pred_picked = keep.tile([P, S], F32)
        nc.vector.tensor_copy(pred_picked[:], pred_kept[:].indirect(ser_t[:]))
        nc.vector.tensor_tensor(lev_t[:].indirect(ser_t[:]), pred_picked[:], obs[:], ALU.add)
        nc.sync.dma_start(out, lev_t[:])
